import numpy as np
import ml_dtypes


def mxq(x, axis, fmt="e4m3"):
    dtype, down = {"e4m3": (ml_dtypes.float8_e4m3fn, 7), "e5m2": (ml_dtypes.float8_e5m2, 14)}[fmt]
    v = np.moveaxis(np.asarray(x, np.float32).astype(ml_dtypes.bfloat16).astype(np.float64), axis, -1)
    blocks = v.reshape(v.shape[:-1] + (-1, 32))
    amax = np.abs(blocks).max(-1, keepdims=True)
    byte = np.maximum(np.where(amax > 0, np.frexp(amax)[1] - 1 + 127, 0) - down, 1)
    scale = np.exp2(byte - 127.0)
    codes = (blocks / scale).astype(np.float32).astype(dtype).astype(np.float64)
    return np.moveaxis((codes * scale).reshape(v.shape), -1, axis)


WIDE = False


def mx_kscale(k):
    if not WIDE:
        return np.ones(k)
    levels = np.array([10, -10, 5, -5, 0])
    if k % 512:
        return np.exp2(np.random.permutation(np.resize(levels, k // 32))).repeat(32)
    a = np.empty((k // 512, 16))
    for p in range(k // 512):
        a[p, :8] = np.random.permutation(np.resize(levels, 8))
        for g in range(8):
            far = levels[np.abs(levels - a[p, g]) >= 10]
            a[p, g + 8] = far[np.random.randint(len(far))]
    return np.exp2(a.ravel()).repeat(32)


def f64(x):
    return np.asarray(x).astype(np.float64)


def striped(idx):
    return np.tile(idx.reshape(-1, 16).T, (8, 1)).astype(np.uint16)


def unstriped(offs):
    return offs[:16].T.reshape(-1).astype(np.int64)


E2M1 = np.array([0.0, 0.5, 1.0, 1.5, 2.0, 3.0, 4.0, 6.0, -0.0, -0.5, -1.0, -1.5, -2.0, -3.0, -4.0, -6.0])


def pack_weight(w, fmt):
    k, n = w.shape
    w = f64(np.asarray(w, np.float32).astype(ml_dtypes.bfloat16)).reshape(k // 32, 32, n)
    amax = np.abs(w).max(1)
    if fmt == "e4m3":
        byte = np.frexp(amax)[1] - 1 + 127 - 7
    else:
        mant, ex = np.frexp(amax / 6.0)
        byte = np.where(mant > 0.5, ex, ex - 1) + 127
    byte = np.clip(np.where(amax > 0, byte, 1), 1, 254)
    scaled = (w * np.exp2(127.0 - byte)[:, None, :]).reshape(k, n).astype(np.float32)
    by_word = np.ascontiguousarray(scaled.reshape(k // 512, 128, 4, n).transpose(0, 1, 3, 2))
    if fmt == "e4m3":
        words = by_word.astype(ml_dtypes.float8_e4m3fn).view(np.uint8)
    else:
        c = by_word.astype(ml_dtypes.float4_e2m1fn).view(np.uint8) & 0xF
        words = (c[..., 0::2] | (c[..., 1::2] << 4)).reshape(k // 512, 128, 2 * n)
    return np.ascontiguousarray(words), np.ascontiguousarray(byte.astype(np.uint8).reshape(k // 512, 16, n))


def unpack_weight(words, scales, fmt):
    g, _, n = scales.shape
    words = np.ascontiguousarray(words).reshape(g, 128, n, -1)
    if fmt == "e4m3":
        vals = words.view(ml_dtypes.float8_e4m3fn).astype(np.float64)
    else:
        nib = np.empty((g, 128, n, 4), np.uint8)
        nib[..., 0::2] = words & 0xF
        nib[..., 1::2] = words >> 4
        vals = E2M1[nib]
    vals = vals * np.repeat(np.exp2(scales.astype(np.float64) - 127.0), 8, axis=1)[..., None]
    return vals.transpose(0, 1, 3, 2).reshape(g * 512, n)


def gelu(v):
    return 0.5 * v * (1.0 + np.tanh(np.sqrt(2.0 / np.pi) * (v + 0.044715 * v**3)))


K, T, E, C, H, N = 1024, 1024, 2, 256, 512, 384


def by_expert(wq, xq):
    return np.concatenate([wq[e].T @ xq[:, e * C:(e + 1) * C] for e in range(E)], axis=1)


def setup_inputs():
    n = np.random.standard_normal
    s = mx_kscale(K)[:, None]
    u = mx_kscale(H)
    w1 = [pack_weight(m, "e2m1") for m in n((E, K, H)) / np.sqrt(K) / s[None]]
    w3 = [pack_weight(m, "e2m1") for m in n((E, K, H)) / np.sqrt(K) / s[None] * u[None, None, :]]
    w2 = [pack_weight(m, "e2m1") for m in n((E, H, N)) / np.sqrt(H) / u[None, :, None]]
    return {
        "xT": (n((K, T)) * s).astype(np.float32),
        "xr": n((N, T)).astype(np.float32),
        "w1_words": np.stack([m[0] for m in w1]),
        "w1_scales": np.stack([m[1] for m in w1]),
        "w3_words": np.stack([m[0] for m in w3]),
        "w3_scales": np.stack([m[1] for m in w3]),
        "w2_words": np.stack([m[0] for m in w2]),
        "w2_scales": np.stack([m[1] for m in w2]),
        "gate": np.tile(np.random.uniform(0.2, 1.0, E * C), (N, 1)).astype(np.float32),
        "offs": striped(np.random.permutation(T)[:E * C]),
    }


def reference(xT, xr, w1_words, w1_scales, w3_words, w3_scales, w2_words, w2_scales, gate, offs):
    idx = unstriped(offs)
    w1 = np.stack([unpack_weight(w1_words[e], w1_scales[e], "e2m1") for e in range(E)])
    w3 = np.stack([unpack_weight(w3_words[e], w3_scales[e], "e2m1") for e in range(E)])
    w2 = np.stack([unpack_weight(w2_words[e], w2_scales[e], "e2m1") for e in range(E)])
    xq = mxq(f64(xT)[:, idx], 0, "e4m3")
    h = gelu(by_expert(w1, xq))
    h = h * by_expert(w3, xq)
    y = by_expert(w2, mxq(h, 0, "e4m3"))
    out = f64(xr).copy()
    out[:, idx] += f64(gate) * y
    return out

@@ -1,0 +1,229 @@
+from contextlib import ExitStack
+
+import concourse.mybir as mybir
+from concourse.masks import make_identity
+
+K, T, E, C, H, N = 1024, 1024, 2, 256, 512, 384
+SLOTS = E * C
+FLOPS = 2 * SLOTS * (2 * K * H + H * N)
+
+F32 = mybir.dt.float32
+BF16 = mybir.dt.bfloat16
+I32 = mybir.dt.int32
+U32 = mybir.dt.uint32
+U16 = mybir.dt.uint16
+U8 = mybir.dt.uint8
+FP8X4 = mybir.dt.float8_e4m3fn_x4
+FP4X4 = mybir.dt.float4_e2m1fn_x4
+MULT = mybir.AluOpType.mult
+ADD = mybir.AluOpType.add
+GELU = mybir.ActivationFunctionType.Gelu_apprx_tanh
+
+P = 128
+PASSES = K // 512
+SLOT_TILES = SLOTS // P
+N_TILES = N // P
+OFFS_COLS = P // 16
+
+
+def tile_moe_res_glu_gelu_kernel(
+    tc, xT, xr, w1_words, w1_scales, w3_words, w3_scales, w2_words, w2_scales, gate, offs, out
+):
+    nc = tc.nc
+    with ExitStack() as ctx:
+        keep = ctx.enter_context(tc.tile_pool(name="keep", bufs=1))
+        work = ctx.enter_context(tc.tile_pool(name="work", bufs=2))
+        psum = ctx.enter_context(tc.psum_pool(name="psum", bufs=1))
+
+        offsets = keep.tile([P, SLOTS // 16], U16, name="offsets")
+        nc.sync.dma_start(offsets[:], offs)
+
+        warm = keep.tile([P, 1], F32, name="warm")
+        nc.gpsimd.memset(warm[:], 0.0)
+        warm_out = keep.tile([P, 1], F32, name="warm_out")
+        nc.scalar.activation(warm_out[:], warm[:], GELU)
+
+        s13 = keep.tile([P, 2 * E * PASSES, H], U8, name="s13", align_bytes=64)
+        s2 = keep.tile([P, E, N], U8, name="s2", align_bytes=64)
+        nc.vector.memset(s13[:].rearrange("p a n -> p (a n)").bitcast(I32), 0)
+        nc.vector.memset(s2[:].rearrange("p a n -> p (a n)").bitcast(I32), 0)
+
+        x_raw = {}
+        def load_x(s, u, t0, t1):
+            rows = xT[s * 512 : (s + 1) * 512, :].rearrange("(p j) t -> p j t", j=4)
+            nc.sync.dma_start(x_raw[s, u][:, :, t0:t1], rows[:, 2 * u : 2 * u + 2, t0:t1])
+        for s in range(PASSES):
+            for u in range(2):
+                x_raw[s, u] = keep.tile([P, 2, T], F32, name=f"x_raw{s}{u}")
+
+        w1 = [keep.tile([P, PASSES, 2 * H], U8, name=f"w1_{e}", align_bytes=64) for e in range(E)]
+        w3 = [keep.tile([P, PASSES, 2 * H], U8, name=f"w3_{e}", align_bytes=64) for e in range(E)]
+        w2 = keep.tile([P, E, 2 * N], U8, name="w2", align_bytes=64)
+        gate_sb = keep.tile([P, N_TILES, SLOTS], F32, name="gate_sb")
+        xr_sb = [keep.tile([P, T], F32, name=f"xr{n}") for n in range(N_TILES)]
+
+        def load_w(tile, words):
+            nc.sync.dma_start(tile[:].bitcast(I32), words.bitcast(I32))
+
+        load_x(0, 0, 0, T)
+        load_x(0, 1, 0, T)
+        for q in range(4):
+            for a, scales in ((0, w1_scales), (1, w3_scales)):
+                nc.scalar.dma_start(
+                    s13[32 * q : 32 * q + 4, a * E * PASSES : (a + 1) * E * PASSES, :].bitcast(I32),
+                    scales[:, :, 4 * q : 4 * q + 4, :].rearrange("e s q n -> q (e s) n").bitcast(I32),
+                )
+        load_x(1, 0, 0, T)
+        load_w(w1[0], w1_words[0].rearrange("s p b -> p s b"))
+        load_w(w3[0], w3_words[0].rearrange("s p b -> p s b"))
+        load_x(1, 1, 0, T // 2)
+        load_x(1, 1, T // 2, T)
+        load_w(w1[1], w1_words[1].rearrange("s p b -> p s b"))
+        load_w(w3[1], w3_words[1].rearrange("s p b -> p s b"))
+        load_w(w2, w2_words.rearrange("e s p b -> p (e s) b"))
+        for q in range(4):
+            nc.sync.dma_start(
+                s2[32 * q : 32 * q + 4, :, :].bitcast(I32),
+                w2_scales[:, :, 4 * q : 4 * q + 4, :].rearrange("e s q n -> q (e s) n").bitcast(I32),
+            )
+        nc.sync.dma_start(gate_sb[:], gate.rearrange("(c p) s -> p c s", p=P))
+        for n in range(N_TILES):
+            nc.sync.dma_start(xr_sb[n][:], xr[n * P : (n + 1) * P, :])
+
+        identity = keep.tile([P, P], F32, name="identity")
+        make_identity(nc, identity[:])
+        routed = [keep.tile([P, T], F32, name=f"routed{n}") for n in range(N_TILES)]
+        for n in range(N_TILES):
+            nc.gpsimd.memset(routed[n][:], 0.0)
+
+        x_grp = [keep.tile([P, SLOTS, 4], BF16, name=f"x_grp{s}", align_bytes=64) for s in range(PASSES)]
+        x_codes = [keep.tile([P, SLOTS], U32, name=f"x_codes{s}", align_bytes=64) for s in range(PASSES)]
+        x_scales = [keep.tile([P, SLOTS], U8, name=f"x_scales{s}", align_bytes=64) for s in range(PASSES)]
+        pairs = {}
+        for s in range(PASSES):
+            for u in range(2):
+                pairs[s, u] = keep.tile([P, T, 2], BF16, name=f"pairs{s}{u}", align_bytes=64)
+
+        def cast(engine, s, u, t0, t1):
+            src = x_raw[s, u][:, :, t0:t1].rearrange("p j t -> p t j")
+            dst = pairs[s, u][:, t0:t1, :]
+            if engine == "scalar":
+                nc.scalar.copy(dst, src)
+            else:
+                nc.vector.tensor_copy(dst, src)
+
+        def gather(s, u, j0, j1):
+            words = x_grp[s][:].rearrange("p t d -> p (t d)").bitcast(U32).rearrange("p (t u) -> p u t", u=2)
+            nc.vector.tensor_copy(
+                words[:, u, j0:j1],
+                pairs[s, u][:].rearrange("p t j -> p (t j)").bitcast(U32).indirect(offsets[:, j0 // 16 : j1 // 16]),
+            )
+
+        def quantise_x(s, j0, j1):
+            nc.vector.quantize_mx(
+                out=x_codes[s][:, j0:j1].bitcast(FP8X4),
+                scales=x_scales[s][:, j0:j1],
+                in_=x_grp[s][:, j0:j1, :].rearrange("p t d -> p (t d)"),
+            )
+
+        SPLIT = 736
+        cast("scalar", 0, 0, 0, SPLIT)
+        cast("vector", 0, 0, SPLIT, T)
+        gather(0, 0, 0, SLOTS)
+        cast("scalar", 0, 1, 0, SPLIT)
+        cast("vector", 0, 1, SPLIT, T)
+        gather(0, 1, 0, SLOTS)
+        quantise_x(0, 0, SLOTS)
+        cast("scalar", 1, 0, 0, SPLIT)
+        cast("vector", 1, 0, SPLIT, T)
+        gather(1, 0, 0, SLOTS)
+        cast("scalar", 1, 1, 0, T // 2)
+        LAST = T // 2 + 192
+        cast("scalar", 1, 1, T // 2, LAST)
+        cast("vector", 1, 1, LAST, T)
+        for e in range(E):
+            gather(1, 1, e * C, (e + 1) * C)
+            quantise_x(1, e * C, (e + 1) * C)
+
+        a_bank = [psum.tile([P, H], F32, name=f"a{i}") for i in range(SLOT_TILES)]
+        g_bank = [psum.tile([P, H], F32, name=f"g{i}") for i in range(SLOT_TILES)]
+
+        def first_layer(i, s):
+            e = i * P // C
+            cols = slice(i * P, (i + 1) * P)
+            for bank, words, a in ((a_bank, w1, 0), (g_bank, w3, 1)):
+                nc.tensor.matmul_mx(
+                    out=bank[i][:],
+                    lhsT=x_codes[s][:, cols].bitcast(FP8X4),
+                    lhsT_scale=x_scales[s][:, cols],
+                    rhs=words[e][:, s, :].bitcast(FP4X4),
+                    rhs_scale=s13[:, (a * E + e) * PASSES + s, :],
+                    start=(s == 0),
+                    stop=(s == PASSES - 1),
+                )
+
+        h_tiles = {}
+        def hidden(i):
+            act = work.tile([P, H], F32, name="act")
+            nc.scalar.activation(act[:], a_bank[i][:], GELU)
+            h = work.tile([P, H], BF16, name="h")
+            nc.vector.tensor_tensor(h[:], g_bank[i][:], act[:], MULT)
+            h_tiles[i] = h
+
+        def turn(i):
+            turned = psum.tile([P, 2, P], F32, name=f"turned{i}", tag=f"a{i}")
+            words = h_tiles[i][:].bitcast(F32).rearrange("p (w u) -> p u w", u=2)
+            for u in range(2):
+                nc.tensor.transpose(turned[:, u, :], words[:, u, :], identity[:])
+            h_grp = work.tile([P, P, 4], BF16, name="h_grp", align_bytes=64)
+            nc.scalar.copy(
+                h_grp[:].rearrange("p t d -> p (t d)").bitcast(F32).rearrange("p (t u) -> p t u", u=2),
+                turned[:].rearrange("p u t -> p t u"),
+            )
+            h_codes = work.tile([P, P], U32, name="h_codes", align_bytes=64)
+            h_scales = work.tile([P, P], U8, name="h_scales", align_bytes=64)
+            nc.vector.quantize_mx(
+                out=h_codes[:].bitcast(FP8X4), scales=h_scales[:], in_=h_grp[:].rearrange("p t d -> p (t d)")
+            )
+            return h_codes, h_scales
+
+        def second_layer(i, h_codes, h_scales):
+            e = i * P // C
+            y = psum.tile([P, N_TILES, P], F32, name=f"y{i}", tag=f"g{i}")
+            for n in range(N_TILES):
+                nc.tensor.matmul_mx(
+                    out=y[:, n, :],
+                    lhsT=w2[:, e, 2 * n * P : 2 * (n + 1) * P].bitcast(FP4X4),
+                    lhsT_scale=s2[:, e, n * P : (n + 1) * P],
+                    rhs=h_codes[:].bitcast(FP8X4),
+                    rhs_scale=h_scales[:],
+                    start=True,
+                    stop=True,
+                )
+            gated = work.tile([P, N_TILES, P], F32, name="gated")
+            nc.vector.tensor_tensor(gated[:], y[:], gate_sb[:, :, i * P : (i + 1) * P], MULT)
+            return gated
+
+        def scatter(i, n, gated):
+            nc.vector.tensor_copy(
+                routed[n][:].indirect(offsets[:, i * OFFS_COLS : (i + 1) * OFFS_COLS]), gated[:, n, :]
+            )
+
+        def finish(n):
+            total = keep.tile([P, T], F32, name=f"total{n}")
+            for half in range(2):
+                cols = slice(half * T // 2, (half + 1) * T // 2)
+                nc.vector.tensor_tensor(total[:, cols], routed[n][:, cols], xr_sb[n][:, cols], ADD)
+                nc.sync.dma_start(out[n * P : (n + 1) * P, cols], total[:, cols])
+
+        for i in range(SLOT_TILES):
+            first_layer(i, 0)
+        for i in range(SLOT_TILES):
+            first_layer(i, 1)
+            hidden(i)
+        for i in range(SLOT_TILES):
+            gated = second_layer(i, *turn(i))
+            for n in range(N_TILES):
+                scatter(i, n, gated)
+                if i == SLOT_TILES - 1:
+                    finish(n)

@@ -36,7 +36,6 @@ def tile_moe_res_glu_gelu_kernel(
         psum = ctx.enter_context(tc.psum_pool(name="psum", bufs=1))
 
         offsets = keep.tile([P, SLOTS // 16], U16, name="offsets")
-        nc.sync.dma_start(offsets[:], offs)
 
         warm = keep.tile([P, 1], F32, name="warm")
         nc.gpsimd.memset(warm[:], 0.0)
@@ -65,27 +64,35 @@ def tile_moe_res_glu_gelu_kernel(
         def load_w(tile, words):
             nc.sync.dma_start(tile[:].bitcast(I32), words.bitcast(I32))
 
-        load_x(0, 0, 0, T)
-        load_x(0, 1, 0, T)
+        def load_scales(queue, a, scales, q):
+            queue.dma_start(
+                s13[32 * q : 32 * q + 4, a * E * PASSES : (a + 1) * E * PASSES, :].bitcast(I32),
+                scales[:, :, 4 * q : 4 * q + 4, :].rearrange("e s q n -> q (e s) n").bitcast(I32),
+            )
+        HALF = T // 2
+        nc.sync.dma_start(offsets[:], offs)
+        load_x(0, 0, 0, HALF)
+        load_x(0, 0, HALF, T)
+        load_x(0, 1, 0, HALF)
+        load_x(0, 1, HALF, T)
         for q in range(4):
-            for a, scales in ((0, w1_scales), (1, w3_scales)):
-                nc.scalar.dma_start(
-                    s13[32 * q : 32 * q + 4, a * E * PASSES : (a + 1) * E * PASSES, :].bitcast(I32),
-                    scales[:, :, 4 * q : 4 * q + 4, :].rearrange("e s q n -> q (e s) n").bitcast(I32),
-                )
-        load_x(1, 0, 0, T)
-        load_w(w1[0], w1_words[0].rearrange("s p b -> p s b"))
-        load_w(w3[0], w3_words[0].rearrange("s p b -> p s b"))
-        load_x(1, 1, 0, T // 2)
-        load_x(1, 1, T // 2, T)
-        load_w(w1[1], w1_words[1].rearrange("s p b -> p s b"))
-        load_w(w3[1], w3_words[1].rearrange("s p b -> p s b"))
-        load_w(w2, w2_words.rearrange("e s p b -> p (e s) b"))
+            load_scales(nc.gpsimd, 0, w1_scales, q)
+        for q in range(3):
+            load_scales(nc.sync, 1, w3_scales, q)
+        load_x(1, 0, 0, HALF)
+        load_x(1, 0, HALF, T)
+        load_x(1, 1, 0, HALF)
+        load_x(1, 1, HALF, T)
+        load_scales(nc.sync, 1, w3_scales, 3)
+        for e in range(E):
+            load_w(w1[e], w1_words[e].rearrange("s p b -> p s b"))
+            load_w(w3[e], w3_words[e].rearrange("s p b -> p s b"))
         for q in range(4):
             nc.sync.dma_start(
                 s2[32 * q : 32 * q + 4, :, :].bitcast(I32),
                 w2_scales[:, :, 4 * q : 4 * q + 4, :].rearrange("e s q n -> q (e s) n").bitcast(I32),
             )
+        load_w(w2, w2_words.rearrange("e s p b -> p (e s) b"))
         nc.sync.dma_start(gate_sb[:], gate.rearrange("(c p) s -> p c s", p=P))
         for n in range(N_TILES):
             nc.sync.dma_start(xr_sb[n][:], xr[n * P : (n + 1) * P, :])
@@ -94,7 +101,7 @@ def tile_moe_res_glu_gelu_kernel(
         make_identity(nc, identity[:])
         routed = [keep.tile([P, T], F32, name=f"routed{n}") for n in range(N_TILES)]
         for n in range(N_TILES):
-            nc.gpsimd.memset(routed[n][:], 0.0)
+            nc.vector.memset(routed[n][:], 0.0)
 
         x_grp = [keep.tile([P, SLOTS, 4], BF16, name=f"x_grp{s}", align_bytes=64) for s in range(PASSES)]
         x_codes = [keep.tile([P, SLOTS], U32, name=f"x_codes{s}", align_bytes=64) for s in range(PASSES)]
@@ -126,21 +133,17 @@ def tile_moe_res_glu_gelu_kernel(
                 in_=x_grp[s][:, j0:j1, :].rearrange("p t d -> p (t d)"),
             )
 
-        SPLIT = 736
-        cast("scalar", 0, 0, 0, SPLIT)
-        cast("vector", 0, 0, SPLIT, T)
-        gather(0, 0, 0, SLOTS)
-        cast("scalar", 0, 1, 0, SPLIT)
-        cast("vector", 0, 1, SPLIT, T)
-        gather(0, 1, 0, SLOTS)
-        quantise_x(0, 0, SLOTS)
-        cast("scalar", 1, 0, 0, SPLIT)
-        cast("vector", 1, 0, SPLIT, T)
-        gather(1, 0, 0, SLOTS)
-        cast("scalar", 1, 1, 0, T // 2)
-        LAST = T // 2 + 192
-        cast("scalar", 1, 1, T // 2, LAST)
-        cast("vector", 1, 1, LAST, T)
+        for s in range(PASSES):
+            for u in range(2):
+                last = s == 1 and u == 1
+                split = HALF + (192 if last else 256)
+                cast("scalar", s, u, 0, HALF)
+                cast("scalar", s, u, HALF, split)
+                cast("vector", s, u, split, T)
+                if not last:
+                    gather(s, u, 0, SLOTS)
+            if s == 0:
+                quantise_x(0, 0, SLOTS)
         for e in range(E):
             gather(1, 1, e * C, (e + 1) * C)
             quantise_x(1, e * C, (e + 1) * C)
@@ -162,12 +165,16 @@ def tile_moe_res_glu_gelu_kernel(
                     stop=(s == PASSES - 1),
                 )
 
-        h_tiles = {}
-        def hidden(i):
-            act = work.tile([P, H], F32, name="act")
+        h_tiles, act_tiles, grp_tiles, code_tiles, y_tiles, gated_tiles, turned_tiles = {}, {}, {}, {}, {}, {}, {}
+
+        def activate(i):
+            act = keep.tile([P, H], F32, name=f"act{i}")
             nc.scalar.activation(act[:], a_bank[i][:], GELU)
-            h = work.tile([P, H], BF16, name="h")
-            nc.vector.tensor_tensor(h[:], g_bank[i][:], act[:], MULT)
+            act_tiles[i] = act
+
+        def multiply(i):
+            h = keep.tile([P, H], BF16, name=f"h{i}")
+            nc.vector.tensor_tensor(h[:], g_bank[i][:], act_tiles[i][:], MULT)
             h_tiles[i] = h
 
         def turn(i):
@@ -175,20 +182,30 @@ def tile_moe_res_glu_gelu_kernel(
             words = h_tiles[i][:].bitcast(F32).rearrange("p (w u) -> p u w", u=2)
             for u in range(2):
                 nc.tensor.transpose(turned[:, u, :], words[:, u, :], identity[:])
+            turned_tiles[i] = turned
+
+        def unload(i):
             h_grp = work.tile([P, P, 4], BF16, name="h_grp", align_bytes=64)
-            nc.scalar.copy(
+            copy = nc.vector.tensor_copy if i == 0 else nc.scalar.copy
+            copy(
                 h_grp[:].rearrange("p t d -> p (t d)").bitcast(F32).rearrange("p (t u) -> p t u", u=2),
-                turned[:].rearrange("p u t -> p t u"),
+                turned_tiles[i][:].rearrange("p u t -> p t u"),
             )
+            grp_tiles[i] = h_grp
+
+        def quantise_h(i):
             h_codes = work.tile([P, P], U32, name="h_codes", align_bytes=64)
             h_scales = work.tile([P, P], U8, name="h_scales", align_bytes=64)
             nc.vector.quantize_mx(
-                out=h_codes[:].bitcast(FP8X4), scales=h_scales[:], in_=h_grp[:].rearrange("p t d -> p (t d)")
+                out=h_codes[:].bitcast(FP8X4),
+                scales=h_scales[:],
+                in_=grp_tiles[i][:].rearrange("p t d -> p (t d)"),
             )
-            return h_codes, h_scales
+            code_tiles[i] = (h_codes, h_scales)
 
-        def second_layer(i, h_codes, h_scales):
+        def second_layer(i):
             e = i * P // C
+            h_codes, h_scales = code_tiles[i]
             y = psum.tile([P, N_TILES, P], F32, name=f"y{i}", tag=f"g{i}")
             for n in range(N_TILES):
                 nc.tensor.matmul_mx(
@@ -200,30 +217,74 @@ def tile_moe_res_glu_gelu_kernel(
                     start=True,
                     stop=True,
                 )
-            gated = work.tile([P, N_TILES, P], F32, name="gated")
-            nc.vector.tensor_tensor(gated[:], y[:], gate_sb[:, :, i * P : (i + 1) * P], MULT)
-            return gated
+            y_tiles[i] = y
 
-        def scatter(i, n, gated):
+        def apply_gate(i):
+            gated = keep.tile([P, N_TILES, P], F32, name=f"gated{i}")
+            gates = gate_sb[:, :, i * P : (i + 1) * P]
+            if i > 0:
+                plain = work.tile([P, N_TILES, P], F32, name="plain")
+                nc.scalar.copy(plain[:], y_tiles[i][:])
+                nc.gpsimd.tensor_tensor(gated[:], plain[:], gates, MULT)
+            else:
+                nc.vector.tensor_tensor(gated[:], y_tiles[i][:], gates, MULT)
+            gated_tiles[i] = gated
+
+        def scatter(i, n):
             nc.vector.tensor_copy(
-                routed[n][:].indirect(offsets[:, i * OFFS_COLS : (i + 1) * OFFS_COLS]), gated[:, n, :]
+                routed[n][:].indirect(offsets[:, i * OFFS_COLS : (i + 1) * OFFS_COLS]), gated_tiles[i][:, n, :]
             )
 
         def finish(n):
             total = keep.tile([P, T], F32, name=f"total{n}")
+            engine = nc.gpsimd if n == 0 else nc.vector
             for half in range(2):
                 cols = slice(half * T // 2, (half + 1) * T // 2)
-                nc.vector.tensor_tensor(total[:, cols], routed[n][:, cols], xr_sb[n][:, cols], ADD)
+                engine.tensor_tensor(total[:, cols], routed[n][:, cols], xr_sb[n][:, cols], ADD)
                 nc.sync.dma_start(out[n * P : (n + 1) * P, cols], total[:, cols])
 
-        for i in range(SLOT_TILES):
-            first_layer(i, 0)
-        for i in range(SLOT_TILES):
-            first_layer(i, 1)
-            hidden(i)
-        for i in range(SLOT_TILES):
-            gated = second_layer(i, *turn(i))
-            for n in range(N_TILES):
-                scatter(i, n, gated)
-                if i == SLOT_TILES - 1:
-                    finish(n)
+        first_layer(0, 0)
+        first_layer(1, 0)
+        first_layer(2, 0)
+        first_layer(0, 1)
+        first_layer(3, 0)
+        first_layer(1, 1)
+        first_layer(2, 1)
+        first_layer(3, 1)
+        activate(0)
+        multiply(0)
+        activate(1)
+        multiply(1)
+        turn(0)
+        unload(0)
+        turn(1)
+        quantise_h(0)
+        second_layer(0)
+        activate(2)
+        unload(1)
+        multiply(2)
+        turn(2)
+        activate(3)
+        unload(2)
+        apply_gate(0)
+        quantise_h(1)
+        second_layer(1)
+        apply_gate(1)
+        scatter(0, 0)
+        multiply(3)
+        turn(3)
+        unload(3)
+        quantise_h(2)
+        second_layer(2)
+        apply_gate(2)
+        scatter(0, 1)
+        quantise_h(3)
+        second_layer(3)
+        apply_gate(3)
+        scatter(0, 2)
+        for n in range(N_TILES):
+            scatter(1, n)
+        for n in range(N_TILES):
+            scatter(2, n)
+            scatter(3, n)
+            finish(n)

@@ -62,7 +62,7 @@ def tile_moe_res_glu_gelu_kernel(
         xr_sb = [keep.tile([P, T], F32, name=f"xr{n}") for n in range(N_TILES)]
 
         def load_w(tile, words):
-            nc.sync.dma_start(tile[:].bitcast(I32), words.bitcast(I32))
+            nc.sync.dma_start(tile.bitcast(I32), words.bitcast(I32))
 
         def load_scales(queue, a, scales, q):
             queue.dma_start(
@@ -77,22 +77,25 @@ def tile_moe_res_glu_gelu_kernel(
         load_x(0, 1, HALF, T)
         for q in range(4):
             load_scales(nc.gpsimd, 0, w1_scales, q)
+        load_scales(nc.gpsimd, 1, w3_scales, 3)
         for q in range(3):
             load_scales(nc.sync, 1, w3_scales, q)
         load_x(1, 0, 0, HALF)
         load_x(1, 0, HALF, T)
+        load_w(w1[0][:, 0, :], w1_words[0, 0])
+        load_w(w3[0][:, 0, :], w3_words[0, 0])
         load_x(1, 1, 0, HALF)
         load_x(1, 1, HALF, T)
-        load_scales(nc.sync, 1, w3_scales, 3)
-        for e in range(E):
-            load_w(w1[e], w1_words[e].rearrange("s p b -> p s b"))
-            load_w(w3[e], w3_words[e].rearrange("s p b -> p s b"))
+        load_w(w1[0][:, 1, :], w1_words[0, 1])
+        load_w(w3[0][:, 1, :], w3_words[0, 1])
+        load_w(w1[1][:], w1_words[1].rearrange("s p b -> p s b"))
+        load_w(w3[1][:], w3_words[1].rearrange("s p b -> p s b"))
         for q in range(4):
             nc.sync.dma_start(
                 s2[32 * q : 32 * q + 4, :, :].bitcast(I32),
                 w2_scales[:, :, 4 * q : 4 * q + 4, :].rearrange("e s q n -> q (e s) n").bitcast(I32),
             )
-        load_w(w2, w2_words.rearrange("e s p b -> p (e s) b"))
+        load_w(w2[:], w2_words.rearrange("e s p b -> p (e s) b"))
         nc.sync.dma_start(gate_sb[:], gate.rearrange("(c p) s -> p c s", p=P))
         for n in range(N_TILES):
             nc.sync.dma_start(xr_sb[n][:], xr[n * P : (n + 1) * P, :])
@@ -165,7 +168,7 @@ def tile_moe_res_glu_gelu_kernel(
                     stop=(s == PASSES - 1),
                 )
 
-        h_tiles, act_tiles, grp_tiles, code_tiles, y_tiles, gated_tiles, turned_tiles = {}, {}, {}, {}, {}, {}, {}
+        h_tiles, act_tiles, grp_tiles, code_tiles, y_tiles, turned_tiles = {}, {}, {}, {}, {}, {}
 
         def activate(i):
             act = keep.tile([P, H], F32, name=f"act{i}")
@@ -219,72 +222,63 @@ def tile_moe_res_glu_gelu_kernel(
                 )
             y_tiles[i] = y
 
-        def apply_gate(i):
-            gated = keep.tile([P, N_TILES, P], F32, name=f"gated{i}")
-            gates = gate_sb[:, :, i * P : (i + 1) * P]
-            if i > 0:
-                plain = work.tile([P, N_TILES, P], F32, name="plain")
-                nc.scalar.copy(plain[:], y_tiles[i][:])
-                nc.gpsimd.tensor_tensor(gated[:], plain[:], gates, MULT)
-            else:
-                nc.vector.tensor_tensor(gated[:], y_tiles[i][:], gates, MULT)
-            gated_tiles[i] = gated
+        y_sb = [keep.tile([P, N_TILES, C], F32, name=f"y_sb{e}") for e in range(E)]
 
-        def scatter(i, n):
-            nc.vector.tensor_copy(
-                routed[n][:].indirect(offsets[:, i * OFFS_COLS : (i + 1) * OFFS_COLS]), gated_tiles[i][:, n, :]
+        def unload_y(i):
+            first = i * P % C
+            nc.scalar.copy(y_sb[i * P // C][:, :, first : first + P], y_tiles[i][:])
+
+        def scatter(first, count, n):
+            e, c0 = first // C, first % C
+            nc.vector.tensor_tensor(
+                routed[n][:].indirect(offsets[:, first // 16 : (first + count) // 16]),
+                y_sb[e][:, n, c0 : c0 + count],
+                gate_sb[:, n, first : first + count],
+                MULT,
             )
 
         def finish(n):
             total = keep.tile([P, T], F32, name=f"total{n}")
-            engine = nc.gpsimd if n == 0 else nc.vector
             for half in range(2):
                 cols = slice(half * T // 2, (half + 1) * T // 2)
-                engine.tensor_tensor(total[:, cols], routed[n][:, cols], xr_sb[n][:, cols], ADD)
+                nc.vector.tensor_tensor(total[:, cols], routed[n][:, cols], xr_sb[n][:, cols], ADD)
                 nc.sync.dma_start(out[n * P : (n + 1) * P, cols], total[:, cols])
 
-        first_layer(0, 0)
-        first_layer(1, 0)
-        first_layer(2, 0)
-        first_layer(0, 1)
-        first_layer(3, 0)
-        first_layer(1, 1)
-        first_layer(2, 1)
-        first_layer(3, 1)
+        for i, s in ((0, 0), (1, 0), (2, 0), (0, 1), (1, 1), (3, 0), (2, 1), (3, 1)):
+            first_layer(i, s)
         activate(0)
-        multiply(0)
         activate(1)
-        multiply(1)
+        multiply(0)
         turn(0)
-        unload(0)
+        multiply(1)
         turn(1)
+        unload(0)
         quantise_h(0)
-        second_layer(0)
         activate(2)
-        unload(1)
-        multiply(2)
-        turn(2)
         activate(3)
-        unload(2)
-        apply_gate(0)
-        quantise_h(1)
-        second_layer(1)
-        apply_gate(1)
-        scatter(0, 0)
+        second_layer(0)
+        multiply(2)
+        unload(1)
         multiply(3)
+        turn(2)
+        unload_y(0)
+        quantise_h(1)
+        scatter(0, P, 0)
         turn(3)
+        second_layer(1)
+        scatter(0, P, 1)
+        unload(2)
         unload(3)
+        scatter(0, P, 2)
         quantise_h(2)
+        unload_y(1)
         second_layer(2)
-        apply_gate(2)
-        scatter(0, 1)
+        unload_y(2)
         quantise_h(3)
         second_layer(3)
-        apply_gate(3)
-        scatter(0, 2)
         for n in range(N_TILES):
-            scatter(1, n)
+            scatter(P, P, n)
+        unload_y(3)
         for n in range(N_TILES):
-            scatter(2, n)
-            scatter(3, n)
+            scatter(C, C, n)
             finish(n)

@@ -71,15 +71,16 @@ def tile_moe_res_glu_gelu_kernel(
             )
         HALF = T // 2
         nc.sync.dma_start(offsets[:], offs)
-        load_x(0, 0, 0, HALF)
-        load_x(0, 0, HALF, T)
+        for quarter in range(4):
+            load_x(0, 0, quarter * T // 4, (quarter + 1) * T // 4)
         load_x(0, 1, 0, HALF)
         load_x(0, 1, HALF, T)
         for q in range(4):
             load_scales(nc.gpsimd, 0, w1_scales, q)
         load_scales(nc.gpsimd, 1, w3_scales, 3)
-        for q in range(3):
-            load_scales(nc.sync, 1, w3_scales, q)
+        load_scales(nc.sync, 1, w3_scales, 0)
+        load_scales(nc.gpsimd, 1, w3_scales, 1)
+        load_scales(nc.gpsimd, 1, w3_scales, 2)
         load_x(1, 0, 0, HALF)
         load_x(1, 0, HALF, T)
         load_w(w1[0][:, 0, :], w1_words[0, 0])
@@ -136,20 +137,24 @@ def tile_moe_res_glu_gelu_kernel(
                 in_=x_grp[s][:, j0:j1, :].rearrange("p t d -> p (t d)"),
             )
 
-        for s in range(PASSES):
-            for u in range(2):
-                last = s == 1 and u == 1
-                split = HALF + (192 if last else 256)
-                cast("scalar", s, u, 0, HALF)
-                cast("scalar", s, u, HALF, split)
-                cast("vector", s, u, split, T)
-                if not last:
-                    gather(s, u, 0, SLOTS)
-            if s == 0:
-                quantise_x(0, 0, SLOTS)
-        for e in range(E):
-            gather(1, 1, e * C, (e + 1) * C)
-            quantise_x(1, e * C, (e + 1) * C)
+        QUARTER = T // 4
+        cast("scalar", 0, 0, 0, QUARTER)
+        cast("vector", 0, 0, QUARTER, 2 * QUARTER)
+        cast("scalar", 0, 0, 2 * QUARTER, 3 * QUARTER)
+        cast("vector", 0, 0, 3 * QUARTER, T)
+        gather(0, 0, 0, SLOTS)
+        cast("scalar", 0, 1, 0, HALF)
+        cast("scalar", 0, 1, HALF, HALF + 128)
+        cast("vector", 0, 1, HALF + 128, T)
+        gather(0, 1, 0, SLOTS)
+        cast("scalar", 1, 0, 0, HALF)
+        cast("scalar", 1, 0, HALF, HALF + 320)
+        cast("vector", 1, 0, HALF + 320, T)
+        quantise_x(0, 0, SLOTS)
+        gather(1, 0, 0, SLOTS)
+        cast("scalar", 1, 1, 0, HALF)
+        cast("scalar", 1, 1, HALF, HALF + 128)
+        cast("vector", 1, 1, HALF + 128, T)
 
         a_bank = [psum.tile([P, H], F32, name=f"a{i}") for i in range(SLOT_TILES)]
         g_bank = [psum.tile([P, H], F32, name=f"g{i}") for i in range(SLOT_TILES)]
@@ -237,48 +242,113 @@ def tile_moe_res_glu_gelu_kernel(
                 MULT,
             )
 
-        def finish(n):
-            total = keep.tile([P, T], F32, name=f"total{n}")
-            for half in range(2):
-                cols = slice(half * T // 2, (half + 1) * T // 2)
-                nc.vector.tensor_tensor(total[:, cols], routed[n][:, cols], xr_sb[n][:, cols], ADD)
-                nc.sync.dma_start(out[n * P : (n + 1) * P, cols], total[:, cols])
+        totals = [keep.tile([P, T], F32, name=f"total{n}") for n in range(N_TILES)]
 
-        for i, s in ((0, 0), (1, 0), (2, 0), (0, 1), (1, 1), (3, 0), (2, 1), (3, 1)):
-            first_layer(i, s)
+        def add_and_store(n, c0, c1):
+            cols = slice(c0, c1)
+            nc.vector.tensor_tensor(totals[n][:, cols], routed[n][:, cols], xr_sb[n][:, cols], ADD)
+            nc.sync.dma_start(out[n * P : (n + 1) * P, cols], totals[n][:, cols])
+
+        sum_banks, sums, back_banks = {}, {}, {}
+
+        def sum_transposed(source, bank, c0, blocks, first):
+            for b in range(blocks):
+                nc.tensor.matmul(
+                    bank[:, b, :],
+                    source[:, c0 + b * P : c0 + (b + 1) * P],
+                    identity[:],
+                    start=(first and b == 0),
+                    stop=(not first and b == blocks - 1),
+                    is_transpose=True,
+                )
+
+        def sum_residual(n, c0, blocks, tag):
+            bank = psum.tile([P, blocks, P], F32, name=f"sum{n}_{c0}", tag=f"a{tag}")
+            sum_banks[n, c0] = bank
+            sum_transposed(xr_sb[n], bank, c0, blocks, True)
+
+        def sum_routed(n, c0, blocks):
+            sum_transposed(routed[n], sum_banks[n, c0], c0, blocks, False)
+
+        def unload_sum(n, c0, blocks):
+            total = keep.tile([P, blocks, P], F32, name=f"sumT{n}_{c0}")
+            nc.scalar.copy(total[:], sum_banks[n, c0][:])
+            sums[n, c0] = total
+
+        def turn_back(n, c0, blocks, tag):
+            bank = psum.tile([P, blocks, P], F32, name=f"back{n}_{c0}", tag=f"g{tag}")
+            for b in range(blocks):
+                nc.tensor.transpose(bank[:, b, :], sums[n, c0][:, b, :], identity[:])
+            back_banks[n, c0] = bank
+
+        def store_sum(n, c0, blocks):
+            cols = slice(c0, c0 + blocks * P)
+            nc.scalar.copy(totals[n][:, cols], back_banks[n, c0][:].rearrange("p b t -> p (b t)"))
+            nc.scalar.dma_start(out[n * P : (n + 1) * P, cols], totals[n][:, cols])
+
+        first_layer(0, 0)
+        first_layer(1, 0)
+        first_layer(2, 0)
+        gather(1, 1, 0, C)
+        quantise_x(1, 0, C)
+        gather(1, 1, C, SLOTS)
+        first_layer(0, 1)
         activate(0)
+        first_layer(1, 1)
+        first_layer(3, 0)
         activate(1)
+        quantise_x(1, C, SLOTS)
+        first_layer(2, 1)
+        activate(2)
         multiply(0)
         turn(0)
         multiply(1)
-        turn(1)
         unload(0)
-        quantise_h(0)
-        activate(2)
+        first_layer(3, 1)
+        turn(1)
         activate(3)
-        second_layer(0)
+        quantise_h(0)
         multiply(2)
         unload(1)
+        quantise_h(1)
+        second_layer(0)
         multiply(3)
         turn(2)
         unload_y(0)
-        quantise_h(1)
-        scatter(0, P, 0)
-        turn(3)
-        second_layer(1)
-        scatter(0, P, 1)
         unload(2)
-        unload(3)
-        scatter(0, P, 2)
+        second_layer(1)
+        turn(3)
+        scatter(0, P, 0)
         quantise_h(2)
         unload_y(1)
+        unload(3)
+        scatter(P, P, 0)
         second_layer(2)
         unload_y(2)
         quantise_h(3)
         second_layer(3)
-        for n in range(N_TILES):
-            scatter(P, P, n)
+        scatter(0, C, 1)
         unload_y(3)
-        for n in range(N_TILES):
-            scatter(C, C, n)
-            finish(n)
+        sum_residual(0, 0, 4, 0)
+        sum_residual(0, HALF, 4, 1)
+        sum_residual(1, 0, 2, 2)
+        scatter(C, C, 0)
+        sum_routed(0, 0, 4)
+        unload_sum(0, 0, 4)
+        sum_routed(0, HALF, 4)
+        unload_sum(0, HALF, 4)
+        scatter(C, C, 1)
+        turn_back(0, 0, 4, 0)
+        store_sum(0, 0, 4)
+        turn_back(0, HALF, 4, 1)
+        store_sum(0, HALF, 4)
+        scatter(0, C, 2)
+        sum_routed(1, 0, 2)
+        unload_sum(1, 0, 2)
+        turn_back(1, 0, 2, 2)
+        store_sum(1, 0, 2)
+        add_and_store(1, 256, 768)
+        scatter(C, C, 2)
+        add_and_store(1, 768, T)
+        add_and_store(2, 0, HALF)
+        add_and_store(2, HALF, T)

from contextlib import ExitStack

import concourse.mybir as mybir
from concourse.masks import make_identity

K, T, E, C, H, N = 1024, 1024, 2, 256, 512, 384
SLOTS = E * C
FLOPS = 2 * SLOTS * (2 * K * H + H * N)

F32 = mybir.dt.float32
BF16 = mybir.dt.bfloat16
I32 = mybir.dt.int32
U32 = mybir.dt.uint32
U16 = mybir.dt.uint16
U8 = mybir.dt.uint8
FP8X4 = mybir.dt.float8_e4m3fn_x4
FP4X4 = mybir.dt.float4_e2m1fn_x4
MULT = mybir.AluOpType.mult
ADD = mybir.AluOpType.add
GELU = mybir.ActivationFunctionType.Gelu_apprx_tanh

P = 128
PASSES = K // 512
SLOT_TILES = SLOTS // P
N_TILES = N // P
OFFS_COLS = P // 16


def tile_moe_res_glu_gelu_kernel(
    tc, xT, xr, w1_words, w1_scales, w3_words, w3_scales, w2_words, w2_scales, gate, offs, out
):
    nc = tc.nc
    with ExitStack() as ctx:
        keep = ctx.enter_context(tc.tile_pool(name="keep", bufs=1))
        work = ctx.enter_context(tc.tile_pool(name="work", bufs=2))
        psum = ctx.enter_context(tc.psum_pool(name="psum", bufs=1))

        offsets = keep.tile([P, SLOTS // 16], U16, name="offsets")

        warm = keep.tile([P, 1], F32, name="warm")
        nc.gpsimd.memset(warm[:], 0.0)
        warm_out = keep.tile([P, 1], F32, name="warm_out")
        nc.scalar.activation(warm_out[:], warm[:], GELU)

        s13 = keep.tile([P, 2 * E * PASSES, H], U8, name="s13", align_bytes=64)
        s2 = keep.tile([P, E, N], U8, name="s2", align_bytes=64)
        nc.vector.memset(s13[:].rearrange("p a n -> p (a n)").bitcast(I32), 0)
        nc.vector.memset(s2[:].rearrange("p a n -> p (a n)").bitcast(I32), 0)

        x_raw = {}
        def load_x(s, u, t0, t1):
            rows = xT[s * 512 : (s + 1) * 512, :].rearrange("(p j) t -> p j t", j=4)
            nc.sync.dma_start(x_raw[s, u][:, :, t0:t1], rows[:, 2 * u : 2 * u + 2, t0:t1])
        for s in range(PASSES):
            for u in range(2):
                x_raw[s, u] = keep.tile([P, 2, T], F32, name=f"x_raw{s}{u}")

        w1 = [keep.tile([P, PASSES, 2 * H], U8, name=f"w1_{e}", align_bytes=64) for e in range(E)]
        w3 = [keep.tile([P, PASSES, 2 * H], U8, name=f"w3_{e}", align_bytes=64) for e in range(E)]
        w2 = keep.tile([P, E, 2 * N], U8, name="w2", align_bytes=64)
        gate_sb = keep.tile([P, N_TILES, SLOTS], F32, name="gate_sb")
        xr_sb = [keep.tile([P, T], F32, name=f"xr{n}") for n in range(N_TILES)]

        def load_w(tile, words):
            nc.sync.dma_start(tile.bitcast(I32), words.bitcast(I32))

        def load_scales(queue, a, scales, q):
            queue.dma_start(
                s13[32 * q : 32 * q + 4, a * E * PASSES : (a + 1) * E * PASSES, :].bitcast(I32),
                scales[:, :, 4 * q : 4 * q + 4, :].rearrange("e s q n -> q (e s) n").bitcast(I32),
            )
        HALF = T // 2
        nc.sync.dma_start(offsets[:], offs)
        for quarter in range(4):
            load_x(0, 0, quarter * T // 4, (quarter + 1) * T // 4)
        load_x(0, 1, 0, HALF)
        load_x(0, 1, HALF, T)
        for q in range(4):
            load_scales(nc.gpsimd, 0, w1_scales, q)
        load_scales(nc.gpsimd, 1, w3_scales, 3)
        load_scales(nc.sync, 1, w3_scales, 0)
        load_scales(nc.gpsimd, 1, w3_scales, 1)
        load_scales(nc.gpsimd, 1, w3_scales, 2)
        load_x(1, 0, 0, HALF)
        load_x(1, 0, HALF, T)
        load_w(w1[0][:, 0, :], w1_words[0, 0])
        load_w(w3[0][:, 0, :], w3_words[0, 0])
        load_x(1, 1, 0, HALF)
        load_x(1, 1, HALF, T)
        load_w(w1[0][:, 1, :], w1_words[0, 1])
        load_w(w3[0][:, 1, :], w3_words[0, 1])
        load_w(w1[1][:], w1_words[1].rearrange("s p b -> p s b"))
        load_w(w3[1][:], w3_words[1].rearrange("s p b -> p s b"))
        for q in range(4):
            nc.sync.dma_start(
                s2[32 * q : 32 * q + 4, :, :].bitcast(I32),
                w2_scales[:, :, 4 * q : 4 * q + 4, :].rearrange("e s q n -> q (e s) n").bitcast(I32),
            )
        load_w(w2[:], w2_words.rearrange("e s p b -> p (e s) b"))
        nc.sync.dma_start(gate_sb[:], gate.rearrange("(c p) s -> p c s", p=P))
        for n in range(N_TILES):
            nc.sync.dma_start(xr_sb[n][:], xr[n * P : (n + 1) * P, :])

        identity = keep.tile([P, P], F32, name="identity")
        make_identity(nc, identity[:])
        routed = [keep.tile([P, T], F32, name=f"routed{n}") for n in range(N_TILES)]
        for n in range(N_TILES):
            nc.vector.memset(routed[n][:], 0.0)

        x_grp = [keep.tile([P, SLOTS, 4], BF16, name=f"x_grp{s}", align_bytes=64) for s in range(PASSES)]
        x_codes = [keep.tile([P, SLOTS], U32, name=f"x_codes{s}", align_bytes=64) for s in range(PASSES)]
        x_scales = [keep.tile([P, SLOTS], U8, name=f"x_scales{s}", align_bytes=64) for s in range(PASSES)]
        pairs = {}
        for s in range(PASSES):
            for u in range(2):
                pairs[s, u] = keep.tile([P, T, 2], BF16, name=f"pairs{s}{u}", align_bytes=64)

        def cast(engine, s, u, t0, t1):
            src = x_raw[s, u][:, :, t0:t1].rearrange("p j t -> p t j")
            dst = pairs[s, u][:, t0:t1, :]
            if engine == "scalar":
                nc.scalar.copy(dst, src)
            else:
                nc.vector.tensor_copy(dst, src)

        def gather(s, u, j0, j1):
            words = x_grp[s][:].rearrange("p t d -> p (t d)").bitcast(U32).rearrange("p (t u) -> p u t", u=2)
            nc.vector.tensor_copy(
                words[:, u, j0:j1],
                pairs[s, u][:].rearrange("p t j -> p (t j)").bitcast(U32).indirect(offsets[:, j0 // 16 : j1 // 16]),
            )

        def quantise_x(s, j0, j1):
            nc.vector.quantize_mx(
                out=x_codes[s][:, j0:j1].bitcast(FP8X4),
                scales=x_scales[s][:, j0:j1],
                in_=x_grp[s][:, j0:j1, :].rearrange("p t d -> p (t d)"),
            )

        QUARTER = T // 4
        cast("scalar", 0, 0, 0, QUARTER)
        cast("vector", 0, 0, QUARTER, 2 * QUARTER)
        cast("scalar", 0, 0, 2 * QUARTER, 3 * QUARTER)
        cast("vector", 0, 0, 3 * QUARTER, T)
        gather(0, 0, 0, SLOTS)
        cast("scalar", 0, 1, 0, HALF)
        cast("scalar", 0, 1, HALF, HALF + 128)
        cast("vector", 0, 1, HALF + 128, T)
        gather(0, 1, 0, SLOTS)
        cast("scalar", 1, 0, 0, HALF)
        cast("scalar", 1, 0, HALF, HALF + 320)
        cast("vector", 1, 0, HALF + 320, T)
        quantise_x(0, 0, SLOTS)
        gather(1, 0, 0, SLOTS)
        cast("scalar", 1, 1, 0, HALF)
        cast("scalar", 1, 1, HALF, HALF + 128)
        cast("vector", 1, 1, HALF + 128, T)

        a_bank = [psum.tile([P, H], F32, name=f"a{i}") for i in range(SLOT_TILES)]
        g_bank = [psum.tile([P, H], F32, name=f"g{i}") for i in range(SLOT_TILES)]

        def first_layer(i, s):
            e = i * P // C
            cols = slice(i * P, (i + 1) * P)
            for bank, words, a in ((a_bank, w1, 0), (g_bank, w3, 1)):
                nc.tensor.matmul_mx(
                    out=bank[i][:],
                    lhsT=x_codes[s][:, cols].bitcast(FP8X4),
                    lhsT_scale=x_scales[s][:, cols],
                    rhs=words[e][:, s, :].bitcast(FP4X4),
                    rhs_scale=s13[:, (a * E + e) * PASSES + s, :],
                    start=(s == 0),
                    stop=(s == PASSES - 1),
                )

        h_tiles, act_tiles, grp_tiles, code_tiles, y_tiles, turned_tiles = {}, {}, {}, {}, {}, {}

        def activate(i):
            act = keep.tile([P, H], F32, name=f"act{i}")
            nc.scalar.activation(act[:], a_bank[i][:], GELU)
            act_tiles[i] = act

        def multiply(i):
            h = keep.tile([P, H], BF16, name=f"h{i}")
            nc.vector.tensor_tensor(h[:], g_bank[i][:], act_tiles[i][:], MULT)
            h_tiles[i] = h

        def turn(i):
            turned = psum.tile([P, 2, P], F32, name=f"turned{i}", tag=f"a{i}")
            words = h_tiles[i][:].bitcast(F32).rearrange("p (w u) -> p u w", u=2)
            for u in range(2):
                nc.tensor.transpose(turned[:, u, :], words[:, u, :], identity[:])
            turned_tiles[i] = turned

        def unload(i):
            h_grp = work.tile([P, P, 4], BF16, name="h_grp", align_bytes=64)
            copy = nc.vector.tensor_copy if i == 0 else nc.scalar.copy
            copy(
                h_grp[:].rearrange("p t d -> p (t d)").bitcast(F32).rearrange("p (t u) -> p t u", u=2),
                turned_tiles[i][:].rearrange("p u t -> p t u"),
            )
            grp_tiles[i] = h_grp

        def quantise_h(i):
            h_codes = work.tile([P, P], U32, name="h_codes", align_bytes=64)
            h_scales = work.tile([P, P], U8, name="h_scales", align_bytes=64)
            nc.vector.quantize_mx(
                out=h_codes[:].bitcast(FP8X4),
                scales=h_scales[:],
                in_=grp_tiles[i][:].rearrange("p t d -> p (t d)"),
            )
            code_tiles[i] = (h_codes, h_scales)

        def second_layer(i):
            e = i * P // C
            h_codes, h_scales = code_tiles[i]
            y = psum.tile([P, N_TILES, P], F32, name=f"y{i}", tag=f"g{i}")
            for n in range(N_TILES):
                nc.tensor.matmul_mx(
                    out=y[:, n, :],
                    lhsT=w2[:, e, 2 * n * P : 2 * (n + 1) * P].bitcast(FP4X4),
                    lhsT_scale=s2[:, e, n * P : (n + 1) * P],
                    rhs=h_codes[:].bitcast(FP8X4),
                    rhs_scale=h_scales[:],
                    start=True,
                    stop=True,
                )
            y_tiles[i] = y

        y_sb = [keep.tile([P, N_TILES, C], F32, name=f"y_sb{e}") for e in range(E)]

        def unload_y(i):
            first = i * P % C
            nc.scalar.copy(y_sb[i * P // C][:, :, first : first + P], y_tiles[i][:])

        def scatter(first, count, n):
            e, c0 = first // C, first % C
            nc.vector.tensor_tensor(
                routed[n][:].indirect(offsets[:, first // 16 : (first + count) // 16]),
                y_sb[e][:, n, c0 : c0 + count],
                gate_sb[:, n, first : first + count],
                MULT,
            )

        totals = [keep.tile([P, T], F32, name=f"total{n}") for n in range(N_TILES)]

        def add_and_store(n, c0, c1):
            cols = slice(c0, c1)
            nc.vector.tensor_tensor(totals[n][:, cols], routed[n][:, cols], xr_sb[n][:, cols], ADD)
            nc.sync.dma_start(out[n * P : (n + 1) * P, cols], totals[n][:, cols])

        sum_banks, sums, back_banks = {}, {}, {}

        def sum_transposed(source, bank, c0, blocks, first):
            for b in range(blocks):
                nc.tensor.matmul(
                    bank[:, b, :],
                    source[:, c0 + b * P : c0 + (b + 1) * P],
                    identity[:],
                    start=(first and b == 0),
                    stop=(not first and b == blocks - 1),
                    is_transpose=True,
                )

        def sum_residual(n, c0, blocks, tag):
            bank = psum.tile([P, blocks, P], F32, name=f"sum{n}_{c0}", tag=f"a{tag}")
            sum_banks[n, c0] = bank
            sum_transposed(xr_sb[n], bank, c0, blocks, True)

        def sum_routed(n, c0, blocks):
            sum_transposed(routed[n], sum_banks[n, c0], c0, blocks, False)

        def unload_sum(n, c0, blocks):
            total = keep.tile([P, blocks, P], F32, name=f"sumT{n}_{c0}")
            nc.scalar.copy(total[:], sum_banks[n, c0][:])
            sums[n, c0] = total

        def turn_back(n, c0, blocks, tag):
            bank = psum.tile([P, blocks, P], F32, name=f"back{n}_{c0}", tag=f"g{tag}")
            for b in range(blocks):
                nc.tensor.transpose(bank[:, b, :], sums[n, c0][:, b, :], identity[:])
            back_banks[n, c0] = bank

        def store_sum(n, c0, blocks):
            cols = slice(c0, c0 + blocks * P)
            nc.scalar.copy(totals[n][:, cols], back_banks[n, c0][:].rearrange("p b t -> p (b t)"))
            nc.scalar.dma_start(out[n * P : (n + 1) * P, cols], totals[n][:, cols])

        first_layer(0, 0)
        first_layer(1, 0)
        first_layer(2, 0)
        gather(1, 1, 0, C)
        quantise_x(1, 0, C)
        gather(1, 1, C, SLOTS)
        first_layer(0, 1)
        activate(0)
        first_layer(1, 1)
        first_layer(3, 0)
        activate(1)
        quantise_x(1, C, SLOTS)
        first_layer(2, 1)
        activate(2)
        multiply(0)
        turn(0)
        multiply(1)
        unload(0)
        first_layer(3, 1)
        turn(1)
        activate(3)
        quantise_h(0)
        multiply(2)
        unload(1)
        quantise_h(1)
        second_layer(0)
        multiply(3)
        turn(2)
        unload_y(0)
        unload(2)
        second_layer(1)
        turn(3)
        scatter(0, P, 0)
        quantise_h(2)
        unload_y(1)
        unload(3)
        scatter(P, P, 0)
        second_layer(2)
        unload_y(2)
        quantise_h(3)
        second_layer(3)
        scatter(0, C, 1)
        unload_y(3)
        sum_residual(0, 0, 4, 0)
        sum_residual(0, HALF, 4, 1)
        sum_residual(1, 0, 2, 2)
        scatter(C, C, 0)
        sum_routed(0, 0, 4)
        unload_sum(0, 0, 4)
        sum_routed(0, HALF, 4)
        unload_sum(0, HALF, 4)
        scatter(C, C, 1)
        turn_back(0, 0, 4, 0)
        store_sum(0, 0, 4)
        turn_back(0, HALF, 4, 1)
        store_sum(0, HALF, 4)
        scatter(0, C, 2)
        sum_routed(1, 0, 2)
        unload_sum(1, 0, 2)
        turn_back(1, 0, 2, 2)
        store_sum(1, 0, 2)
        add_and_store(1, 256, 768)
        scatter(C, C, 2)
        add_and_store(1, 768, T)
        add_and_store(2, 0, HALF)
        add_and_store(2, HALF, T)
